import numpy as np
import ml_dtypes


def mxq(x, axis, fmt="e4m3"):
    dtype, down = {"e4m3": (ml_dtypes.float8_e4m3fn, 7), "e5m2": (ml_dtypes.float8_e5m2, 14)}[fmt]
    v = np.moveaxis(np.asarray(x, np.float32).astype(ml_dtypes.bfloat16).astype(np.float64), axis, -1)
    blocks = v.reshape(v.shape[:-1] + (-1, 32))
    amax = np.abs(blocks).max(-1, keepdims=True)
    byte = np.maximum(np.where(amax > 0, np.frexp(amax)[1] - 1 + 127, 0) - down, 1)
    scale = np.exp2(byte - 127.0)
    codes = (blocks / scale).astype(np.float32).astype(dtype).astype(np.float64)
    return np.moveaxis((codes * scale).reshape(v.shape), -1, axis)


WIDE = False


def mx_kscale(k):
    if not WIDE:
        return np.ones(k)
    levels = np.array([10, -10, 5, -5, 0])
    if k % 512:
        return np.exp2(np.random.permutation(np.resize(levels, k // 32))).repeat(32)
    a = np.empty((k // 512, 16))
    for p in range(k // 512):
        a[p, :8] = np.random.permutation(np.resize(levels, 8))
        for g in range(8):
            far = levels[np.abs(levels - a[p, g]) >= 10]
            a[p, g + 8] = far[np.random.randint(len(far))]
    return np.exp2(a.ravel()).repeat(32)


def f64(x):
    return np.asarray(x).astype(np.float64)


def striped(idx):
    return np.tile(idx.reshape(-1, 16).T, (8, 1)).astype(np.uint16)


def unstriped(offs):
    return offs[:16].T.reshape(-1).astype(np.int64)


E2M1 = np.array([0.0, 0.5, 1.0, 1.5, 2.0, 3.0, 4.0, 6.0, -0.0, -0.5, -1.0, -1.5, -2.0, -3.0, -4.0, -6.0])


def pack_weight(w, fmt):
    k, n = w.shape
    w = f64(np.asarray(w, np.float32).astype(ml_dtypes.bfloat16)).reshape(k // 32, 32, n)
    amax = np.abs(w).max(1)
    if fmt == "e4m3":
        byte = np.frexp(amax)[1] - 1 + 127 - 7
    else:
        mant, ex = np.frexp(amax / 6.0)
        byte = np.where(mant > 0.5, ex, ex - 1) + 127
    byte = np.clip(np.where(amax > 0, byte, 1), 1, 254)
    scaled = (w * np.exp2(127.0 - byte)[:, None, :]).reshape(k, n).astype(np.float32)
    by_word = np.ascontiguousarray(scaled.reshape(k // 512, 128, 4, n).transpose(0, 1, 3, 2))
    if fmt == "e4m3":
        words = by_word.astype(ml_dtypes.float8_e4m3fn).view(np.uint8)
    else:
        c = by_word.astype(ml_dtypes.float4_e2m1fn).view(np.uint8) & 0xF
        words = (c[..., 0::2] | (c[..., 1::2] << 4)).reshape(k // 512, 128, 2 * n)
    return np.ascontiguousarray(words), np.ascontiguousarray(byte.astype(np.uint8).reshape(k // 512, 16, n))


def unpack_weight(words, scales, fmt):
    g, _, n = scales.shape
    words = np.ascontiguousarray(words).reshape(g, 128, n, -1)
    if fmt == "e4m3":
        vals = words.view(ml_dtypes.float8_e4m3fn).astype(np.float64)
    else:
        nib = np.empty((g, 128, n, 4), np.uint8)
        nib[..., 0::2] = words & 0xF
        nib[..., 1::2] = words >> 4
        vals = E2M1[nib]
    vals = vals * np.repeat(np.exp2(scales.astype(np.float64) - 127.0), 8, axis=1)[..., None]
    return vals.transpose(0, 1, 3, 2).reshape(g * 512, n)


def gelu(v):
    return 0.5 * v * (1.0 + np.tanh(np.sqrt(2.0 / np.pi) * (v + 0.044715 * v**3)))


K, H, T, S, T2, P = 1536, 512, 4096, 1024, 2048, 1024

def setup_inputs():
    n = np.random.standard_normal
    s = mx_kscale(K)[:, None]
    u = mx_kscale(H)[:, None]
    tab_words, tab_scales = pack_weight(n((K, T)) * s, "e4m3")
    wa_words, wa_scales = pack_weight(n((H, H)) / np.sqrt(H) / u * u.T, "e2m1")
    return {
        "tab_words": tab_words, "tab_scales": tab_scales,
        "offs": striped(np.random.permutation(T)[:S]),
        "offs2": striped(np.random.permutation(T2)[:S]),
        "offs3": striped(np.random.permutation(T2)[:P]),
        "offs4": striped(np.random.permutation(T2)[:P]),
        "w1": (n((K, H)) / np.sqrt(K) / s * u.T).astype(np.float32),
        "b1": (0.6 * n(H) * u[:, 0]).astype(np.float32),
        "page0": (n((H, T2)) * u).astype(np.float32),
        "wgs": np.exp(0.3 * n((128, S))).astype(np.float32),
        "hum": (0.8 * n((H, P)) * u).astype(np.float32),
        "wa_words": wa_words, "wa_scales": wa_scales,
        "wb": (n((H, H)) / np.sqrt(H) / u * u.T).astype(np.float32),
        "b2": (0.7 * n(H) * u[:, 0]).astype(np.float32),
        "wgo": np.exp(0.3 * n((128, P))).astype(np.float32),
    }

def reference(tab_words, tab_scales, offs, offs2, offs3, offs4, w1, b1, page0, wgs, hum, wa_words, wa_scales, wb, b2, wgo):
    v = unpack_weight(tab_words, tab_scales, "e4m3")[:, unstriped(offs)]
    h = (mxq(f64(w1), 0, "e4m3").T @ v) + f64(b1)[:, None]
    page = f64(page0).copy()
    page[:, unstriped(offs2)] = np.tile(f64(wgs), (H // 128, 1)) * h
    x = np.abs(page[:, unstriped(offs3)]) + f64(hum)
    xq = mxq(x, 0, "e4m3")
    wa = unpack_weight(wa_words, wa_scales, "e2m1")
    ya = wa.T @ xq
    yb = mxq(f64(wb), 0, "e4m3").T @ xq
    y = np.maximum(ya, yb) + f64(b2)[:, None]
    page[:, unstriped(offs4)] = np.tile(f64(wgo), (H // 128, 1)) * y
    return page

@@ -1,0 +1,311 @@
+from contextlib import ExitStack
+
+import concourse.mybir as mybir
+from concourse.masks import make_identity
+
+K, H, T, S, T2, J = 1536, 512, 4096, 1024, 2048, 1024
+FLOPS = 2 * K * H * S + 2 * 2 * H * H * J
+
+F32 = mybir.dt.float32
+BF16 = mybir.dt.bfloat16
+I32 = mybir.dt.int32
+U32 = mybir.dt.uint32
+U16 = mybir.dt.uint16
+U8 = mybir.dt.uint8
+FP8X4 = mybir.dt.float8_e4m3fn_x4
+FP4X4 = mybir.dt.float4_e2m1fn_x4
+ALU = mybir.AluOpType
+ACT = mybir.ActivationFunctionType
+
+P = 128
+PASSES = K // 512
+BLOCKS = H // P
+HALF = S // 2
+FIRST = 256
+REST = J - FIRST
+
+
+def tile_list_membrane_drying_page_kernel(
+    tc, tab_words, tab_scales, offs, offs2, offs3, offs4, w1, b1, page0, wgs, hum, wa_words, wa_scales, wb, b2, wgo, out
+):
+    nc = tc.nc
+    with ExitStack() as ctx:
+        lists = ctx.enter_context(tc.tile_pool(name="lists", bufs=1))
+        keep = ctx.enter_context(tc.tile_pool(name="keep", bufs=1))
+        ring = ctx.enter_context(tc.tile_pool(name="ring", bufs=2))
+        acc_pool = ctx.enter_context(tc.psum_pool(name="acc", bufs=4))
+        turn_pool = ctx.enter_context(tc.psum_pool(name="turn", bufs=2))
+
+        def held(shape, dtype, name, tag=None):
+            return keep.tile(shape, dtype, name=name, tag=tag or name, align_bytes=64)
+
+        def load_list(source, name):
+            tile = lists.tile([P, S // 16], U16, name=name)
+            nc.sync.dma_start(tile[:], source)
+            return tile
+
+        def entries(list_tile, start, stop):
+            return list_tile[:, start // 16 : stop // 16]
+
+        def load_table(a):
+            tile = held([P, T], U32, f"table{a}")
+            nc.sync.dma_start(tile[:].bitcast(I32), tab_words[a].rearrange("p n t -> p (n t)").bitcast(I32))
+            return tile
+
+        def load_w1(c0, c1):
+            tiles = []
+            for a in range(PASSES):
+                tile = held([P, 4, c1 - c0], F32, f"w1raw{c0}_{a}")
+                nc.sync.dma_start(tile[:], w1[512 * a : 512 * (a + 1), c0:c1].rearrange("(p j) c -> p j c", j=4))
+                tiles.append(tile)
+            return tiles
+
+        def load_page(b):
+            tile = held([P, T2], F32, f"page{b}")
+            nc.sync.dma_start(tile[:], page0[P * b : P * (b + 1), :])
+            return tile
+
+        table_scales = held([P, T], U8, "table_scales")
+        nc.vector.memset(table_scales[:].bitcast(I32), 0)
+        bias_rows = held([P, P], F32, "bias_rows")
+        nc.vector.memset(bias_rows[:], 0.0)
+        nc.gpsimd.dma_start(bias_rows[0:BLOCKS, :], b1.rearrange("(b p) -> b p", p=P))
+        nc.gpsimd.dma_start(bias_rows[BLOCKS : 2 * BLOCKS, :], b2.rearrange("(b p) -> b p", p=P))
+        identity = held([P, P], F32, "identity")
+        make_identity(nc, identity[:])
+        wa_scale = held([P, H], U8, "wa_scale")
+        nc.vector.memset(wa_scale[:].bitcast(I32), 0)
+
+        idx = load_list(offs, "idx")
+        table = [load_table(0)]
+        w1_raw0 = load_w1(0, P)
+        table.append(load_table(1))
+        table.append(load_table(2))
+        wgs_sb = held([P, S], F32, "wgs_sb")
+        nc.sync.dma_start(wgs_sb[:, :HALF], wgs[:, :HALF])
+        page = [load_page(0)]
+        for q in range(4):
+            nc.scalar.dma_start(
+                table_scales[32 * q : 32 * q + 4 * PASSES, :].bitcast(I32), tab_scales[:, 4 * q : 4 * q + 4, :].bitcast(I32)
+            )
+        idx2 = load_list(offs2, "idx2")
+        w1_raw1 = load_w1(P, 2 * P)
+        nc.sync.dma_start(wgs_sb[:, HALF:], wgs[:, HALF:])
+        page.append(load_page(1))
+        w1_raw23 = load_w1(2 * P, 4 * P)
+
+        bias_bank = turn_pool.tile([P, P], F32, name="bias_bank", tag="back")
+        nc.tensor.transpose(bias_bank[:], bias_rows[:], identity[:])
+        bias = held([P, 2 * BLOCKS], F32, "bias")
+        nc.scalar.copy(bias[:], bias_bank[:, : 2 * BLOCKS])
+
+        def round_w1(raw, name):
+            n = raw[0].shape[2] // P
+            grouped = held([P, n, PASSES, 4 * P], BF16, name)
+            for a in range(PASSES):
+                nc.scalar.copy(
+                    grouped[:, :, a, :].rearrange("p n (c i j) -> p n c j i", i=4, j=4),
+                    raw[a][:].rearrange("p j (n c i) -> p n c j i", n=n, i=4),
+                )
+            return grouped
+
+        def quantize(source, name):
+            width = source.shape[1] // 4
+            codes = held([P, width], U32, name + "_codes")
+            scales = held([P, width], U8, name + "_scales")
+            nc.vector.quantize_mx(out=codes[:].bitcast(FP8X4), scales=scales[:], in_=source)
+            return codes, scales
+
+        def quantize_w1(grouped, n, name):
+            return quantize(grouped[:, n, :, :].rearrange("p a w -> p (a w)"), name)
+
+        picked = [held([P, S], U32, f"picked{a}") for a in range(PASSES)]
+        picked_scales = held([P, S], U8, "picked_scales")
+        w1q = [quantize_w1(round_w1(w1_raw0, "w1grp0"), 0, "w1q0")]
+        nc.vector.tensor_copy(picked[0][:], table[0][:].indirect(idx[:]))
+        nc.vector.tensor_copy(picked[1][:], table[1][:].indirect(idx[:]))
+        nc.vector.tensor_copy(picked_scales[:], table_scales[:].indirect(idx[:]))
+        for j0 in (0, HALF):
+            nc.vector.tensor_copy(picked[2][:, j0 : j0 + HALF], table[2][:].indirect(entries(idx, j0, j0 + HALF)))
+
+        wb_raw = held([P, 4, H], F32, "wb_raw", tag="table0")
+        nc.sync.dma_start(wb_raw[:], wb.rearrange("(p j) c -> p j c", j=4))
+        idx3 = load_list(offs3, "idx3")
+        page.append(load_page(2))
+        hum_rows = hum.rearrange("(b p) j -> p b j", p=P)
+        hum_first = held([P, BLOCKS, FIRST], F32, "hum_first")
+        nc.sync.dma_start(hum_first[:], hum_rows[:, :, :FIRST])
+        page.append(load_page(3))
+        idx4 = load_list(offs4, "idx4")
+        wa_codes = held([P, 2 * H], U8, "wa_codes")
+        nc.sync.dma_start(wa_codes[:].bitcast(I32), wa_words[0].bitcast(I32))
+        for q in range(4):
+            nc.sync.dma_start(wa_scale[32 * q : 32 * q + 4, :].bitcast(I32), wa_scales[0, 4 * q : 4 * q + 4, :].bitcast(I32))
+        wgo_sb = held([P, J], F32, "wgo_sb")
+        nc.sync.dma_start(wgo_sb[:], wgo)
+        hum_rest = held([P, BLOCKS, REST], F32, "hum_rest", tag="table2")
+        nc.sync.dma_start(hum_rest[:], hum_rows[:, :, FIRST:])
+
+        def first_product(b, j0):
+            codes, scales = w1q[b]
+            acc = acc_pool.tile([P, HALF], F32, name="acc")
+            for a in range(PASSES):
+                nc.tensor.matmul_mx(
+                    out=acc[:],
+                    lhsT=codes[:, P * a : P * (a + 1)].bitcast(FP8X4),
+                    lhsT_scale=scales[:, P * a : P * (a + 1)],
+                    rhs=picked[a][:, j0 : j0 + HALF].bitcast(FP8X4),
+                    rhs_scale=picked_scales[4 * a :, j0 : j0 + HALF],
+                    start=(a == 0),
+                    stop=(a == PASSES - 1),
+                )
+            return acc
+
+        def add_b1(h, acc, b):
+            nc.scalar.activation(h, acc[:], ACT.Identity, bias=bias[:, b : b + 1])
+
+        def put(b, list_tile, values, weights, j0, j1):
+            nc.vector.tensor_tensor(page[b][:].indirect(entries(list_tile, j0, j1)), values, weights[:, j0:j1], ALU.mult)
+
+        for b, raw, c0 in ((0, w1_raw1, P), (1, w1_raw23, 2 * P)):
+            low, high = first_product(b, 0), first_product(b, HALF)
+            h_low = held([P, HALF], F32, f"h_low{b}")
+            add_b1(h_low[:], low, b)
+            put(b, idx2, h_low[:], wgs_sb, 0, HALF)
+            grouped = round_w1(raw, f"w1grp{c0}")
+            for n in range(grouped.shape[1]):
+                w1q.append(quantize_w1(grouped, n, f"w1q{len(w1q)}"))
+            h_high = held([P, HALF], F32, f"h_high{b}", tag=f"w1raw{c0}_{PASSES - 1}")
+            add_b1(h_high[:], high, b)
+            put(b, idx2, h_high[:], wgs_sb, HALF, S)
+
+        h_whole = {}
+        for b in (2, 3):
+            h_whole[b] = held([P, S], F32, f"h{b}")
+            for j0 in (0, HALF):
+                add_b1(h_whole[b][:, j0 : j0 + HALF], first_product(b, j0), b)
+
+        wb_grouped = held([P, H, 4], BF16, "wb_grouped")
+        for b in range(BLOCKS):
+            nc.scalar.copy(
+                wb_grouped[:, P * b : P * (b + 1), :].rearrange("p (c i) j -> p c j i", i=4),
+                wb_raw[:, :, P * b : P * (b + 1)].rearrange("p j (c i) -> p c j i", i=4),
+            )
+        wb_codes, wb_scales = quantize(wb_grouped[:].rearrange("p c j -> p (c j)"), "wbq")
+
+        put(2, idx2, h_whole[2][:], wgs_sb, 0, S)
+
+        def fetch(dest, b, j0, j1):
+            nc.vector.tensor_copy(dest, page[b][:].indirect(entries(idx3, j0, j1)))
+
+        def join(size, humidity, turned, b):
+            n = size.shape[1] // P
+            bank = turn_pool.tile([P, n, P], F32, name="sum_bank", tag="sum")
+            for jb in range(n):
+                cols = slice(P * jb, P * (jb + 1))
+                nc.tensor.matmul(bank[:, jb, :], humidity[:, cols], identity[:], start=True, stop=False, is_transpose=True)
+                nc.tensor.matmul(bank[:, jb, :], size[:, cols], identity[:], start=False, stop=True, is_transpose=True)
+            nc.scalar.copy(
+                turned[:, :, :, 32 * b : 32 * (b + 1), :],
+                bank[:].rearrange("j n (q u e) -> j n u q e", u=2, e=2),
+            )
+
+        def turn_back(turned, name):
+            n = turned.shape[1]
+            words = turned[:].rearrange("j n u q e -> j (n u q e)").bitcast(F32)
+            grouped = held([P, n * P * 4], BF16, name)
+            grouped_words = grouped[:].bitcast(F32).rearrange("p (n j u) -> p n j u", j=P, u=2)
+            for n0 in range(0, n, 2):
+                bank = turn_pool.tile([P, 2, 2, P], F32, name="back_bank", tag="back")
+                for jb in range(2):
+                    for u in range(2):
+                        w0 = ((n0 + jb) * 2 + u) * P
+                        nc.tensor.transpose(bank[:, jb, u, :], words[:, w0 : w0 + P], identity[:])
+                nc.scalar.copy(grouped_words[:, n0 : n0 + 2, :, :], bank[:].rearrange("p n u j -> p n j u"))
+            return grouped
+
+        got_first = held([P, BLOCKS, FIRST], F32, "got_first", tag="h2")
+        size_first = held([P, BLOCKS, FIRST], F32, "size_first")
+        turned_first = held([P, FIRST // P, 2, P, 2], BF16, "turned_first", tag="table1")
+        for b in range(BLOCKS):
+            if b == BLOCKS - 1:
+                put(b, idx2, h_whole[b][:], wgs_sb, 0, S)
+            fetch(got_first[:, b, :], b, 0, FIRST)
+            nc.scalar.activation(size_first[:, b, :], got_first[:, b, :], ACT.Abs)
+            join(size_first[:, b, :], hum_first[:, b, :], turned_first, b)
+        got_low = held([P, BLOCKS - 1, REST], F32, "got_low", tag="h3")
+        for b in range(BLOCKS - 1):
+            fetch(got_low[:, b, :], b, FIRST, J)
+        x_first = quantize(turn_back(turned_first, "grouped_first")[:], "x_first")
+        got_high = held([P, REST], F32, "got_high", tag="grouped_first")
+        fetch(got_high[:], BLOCKS - 1, FIRST, J)
+
+        def product_a(dest, x, b):
+            nc.tensor.matmul_mx(
+                out=dest,
+                lhsT=wa_codes[:, 2 * P * b : 2 * P * (b + 1)].bitcast(FP4X4),
+                lhsT_scale=wa_scale[:, P * b : P * (b + 1)],
+                rhs=x[0][:].bitcast(FP8X4),
+                rhs_scale=x[1][:],
+                start=True,
+                stop=True,
+            )
+
+        def product_b(dest, x, b):
+            nc.tensor.matmul_mx(
+                out=dest,
+                lhsT=wb_codes[:, P * b : P * (b + 1)].bitcast(FP8X4),
+                lhsT_scale=wb_scales[:, P * b : P * (b + 1)],
+                rhs=x[0][:].bitcast(FP8X4),
+                rhs_scale=x[1][:],
+                start=True,
+                stop=True,
+            )
+
+        def scores(x, b):
+            width = x[0].shape[1]
+            if 2 * width <= 512:
+                bank = acc_pool.tile([P, 2, width], F32, name="acc")
+                ya, yb = bank[:, 0, :], bank[:, 1, :]
+            else:
+                bank_a = acc_pool.tile([P, width], F32, name="acc")
+                bank_b = acc_pool.tile([P, width], F32, name="acc")
+                ya, yb = bank_a[:], bank_b[:]
+            product_a(ya, x, b)
+            product_b(yb, x, b)
+            ya_sb = ring.tile([P, width], F32, name=f"ya_sb{width}")
+            nc.scalar.activation(ya_sb[:], ya, ACT.Identity, bias=bias[:, BLOCKS + b : BLOCKS + b + 1])
+            return ya_sb, yb
+
+        def larger(y, pair, b):
+            ya_sb, yb = pair
+            nc.vector.scalar_tensor_tensor(y, yb, bias[:, BLOCKS + b : BLOCKS + b + 1], ya_sb[:], ALU.add, ALU.max)
+
+        size_rest = held([P, BLOCKS, REST], F32, "size_rest", tag="table1")
+
+        def make_x(j0, j1, name):
+            cols = slice(j0 - FIRST, j1 - FIRST)
+            turned = held([P, (j1 - j0) // P, 2, P, 2], BF16, "turned_" + name)
+            for b in range(BLOCKS):
+                got = got_low[:, b, cols] if b < BLOCKS - 1 else got_high[:, cols]
+                nc.scalar.activation(size_rest[:, b, cols], got, ACT.Abs)
+                join(size_rest[:, b, cols], hum_rest[:, b, cols], turned, b)
+            return quantize(turn_back(turned, "grouped_" + name)[:], "x_" + name)
+
+        x = x_first
+        for j0, j1, j2, name in ((0, FIRST, 2 * FIRST, "mid"), (FIRST, 2 * FIRST, J, "end")):
+            for b in range(BLOCKS - 1):
+                y = ring.tile([P, j1 - j0], F32, name="y_early")
+                larger(y[:], scores(x, b), b)
+                put(b, idx4, y[:], wgo_sb, j0, j1)
+            last = scores(x, BLOCKS - 1)
+            x = make_x(j1, j2, name)
+            y = held([P, j1 - j0], F32, "y_before_" + name, tag="grouped_" + name)
+            larger(y[:], last, BLOCKS - 1)
+            put(BLOCKS - 1, idx4, y[:], wgo_sb, j0, j1)
+
+        for b in range(BLOCKS):
+            y = ring.tile([P, J - 2 * FIRST], F32, name="y_late")
+            larger(y[:], scores(x, b), b)
+            put(b, idx4, y[:], wgo_sb, 2 * FIRST, J)
+            nc.sync.dma_start(out[P * b : P * (b + 1), :], page[b][:])

@@ -21,8 +21,7 @@ P = 128
 PASSES = K // 512
 BLOCKS = H // P
 HALF = S // 2
-FIRST = 256
-REST = J - FIRST
+RUN = 256
 
 
 def tile_list_membrane_drying_page_kernel(
@@ -32,7 +31,7 @@ def tile_list_membrane_drying_page_kernel(
     with ExitStack() as ctx:
         lists = ctx.enter_context(tc.tile_pool(name="lists", bufs=1))
         keep = ctx.enter_context(tc.tile_pool(name="keep", bufs=1))
-        ring = ctx.enter_context(tc.tile_pool(name="ring", bufs=2))
+        ring = ctx.enter_context(tc.tile_pool(name="ring", bufs=4))
         acc_pool = ctx.enter_context(tc.psum_pool(name="acc", bufs=4))
         turn_pool = ctx.enter_context(tc.psum_pool(name="turn", bufs=2))
 
@@ -65,14 +64,16 @@ def tile_list_membrane_drying_page_kernel(
             nc.sync.dma_start(tile[:], page0[P * b : P * (b + 1), :])
             return tile
 
-        table_scales = held([P, T], U8, "table_scales")
-        nc.vector.memset(table_scales[:].bitcast(I32), 0)
-        bias_rows = held([P, P], F32, "bias_rows")
-        nc.vector.memset(bias_rows[:], 0.0)
-        nc.gpsimd.dma_start(bias_rows[0:BLOCKS, :], b1.rearrange("(b p) -> b p", p=P))
-        nc.gpsimd.dma_start(bias_rows[BLOCKS : 2 * BLOCKS, :], b2.rearrange("(b p) -> b p", p=P))
         identity = held([P, P], F32, "identity")
         make_identity(nc, identity[:])
+        table_scales = held([P, T], U8, "table_scales")
+        nc.vector.memset(table_scales[:].bitcast(I32), 0)
+        for q in range(4):
+            nc.gpsimd.dma_start(
+                table_scales[32 * q : 32 * q + 4 * PASSES, :].bitcast(I32), tab_scales[:, 4 * q : 4 * q + 4, :].bitcast(I32)
+            )
+        bias_rows = held([P, P], F32, "bias_rows")
+        nc.vector.memset(bias_rows[:], 0.0)
         wa_scale = held([P, H], U8, "wa_scale")
         nc.vector.memset(wa_scale[:].bitcast(I32), 0)
 
@@ -84,10 +85,8 @@ def tile_list_membrane_drying_page_kernel(
         wgs_sb = held([P, S], F32, "wgs_sb")
         nc.sync.dma_start(wgs_sb[:, :HALF], wgs[:, :HALF])
         page = [load_page(0)]
-        for q in range(4):
-            nc.scalar.dma_start(
-                table_scales[32 * q : 32 * q + 4 * PASSES, :].bitcast(I32), tab_scales[:, 4 * q : 4 * q + 4, :].bitcast(I32)
-            )
+        nc.scalar.dma_start(bias_rows[0:BLOCKS, :], b1.rearrange("(b p) -> b p", p=P))
+        nc.scalar.dma_start(bias_rows[BLOCKS : 2 * BLOCKS, :], b2.rearrange("(b p) -> b p", p=P))
         idx2 = load_list(offs2, "idx2")
         w1_raw1 = load_w1(P, 2 * P)
         nc.sync.dma_start(wgs_sb[:, HALF:], wgs[:, HALF:])
@@ -119,12 +118,13 @@ def tile_list_membrane_drying_page_kernel(
         def quantize_w1(grouped, n, name):
             return quantize(grouped[:, n, :, :].rearrange("p a w -> p (a w)"), name)
 
-        picked = [held([P, S], U32, f"picked{a}") for a in range(PASSES)]
+        picked = [held([P, S], U32, f"picked{a}") for a in range(PASSES - 1)]
         picked_scales = held([P, S], U8, "picked_scales")
         w1q = [quantize_w1(round_w1(w1_raw0, "w1grp0"), 0, "w1q0")]
         nc.vector.tensor_copy(picked[0][:], table[0][:].indirect(idx[:]))
         nc.vector.tensor_copy(picked[1][:], table[1][:].indirect(idx[:]))
         nc.vector.tensor_copy(picked_scales[:], table_scales[:].indirect(idx[:]))
+        picked.append(held([P, S], U32, "picked2", tag="table_scales"))
         for j0 in (0, HALF):
             nc.vector.tensor_copy(picked[2][:, j0 : j0 + HALF], table[2][:].indirect(entries(idx, j0, j0 + HALF)))
 
@@ -133,8 +133,8 @@ def tile_list_membrane_drying_page_kernel(
         idx3 = load_list(offs3, "idx3")
         page.append(load_page(2))
         hum_rows = hum.rearrange("(b p) j -> p b j", p=P)
-        hum_first = held([P, BLOCKS, FIRST], F32, "hum_first")
-        nc.sync.dma_start(hum_first[:], hum_rows[:, :, :FIRST])
+        hum_low = held([P, BLOCKS, HALF], F32, "hum_low")
+        nc.sync.dma_start(hum_low[:], hum_rows[:, :, :HALF])
         page.append(load_page(3))
         idx4 = load_list(offs4, "idx4")
         wa_codes = held([P, 2 * H], U8, "wa_codes")
@@ -143,8 +143,8 @@ def tile_list_membrane_drying_page_kernel(
             nc.sync.dma_start(wa_scale[32 * q : 32 * q + 4, :].bitcast(I32), wa_scales[0, 4 * q : 4 * q + 4, :].bitcast(I32))
         wgo_sb = held([P, J], F32, "wgo_sb")
         nc.sync.dma_start(wgo_sb[:], wgo)
-        hum_rest = held([P, BLOCKS, REST], F32, "hum_rest", tag="table2")
-        nc.sync.dma_start(hum_rest[:], hum_rows[:, :, FIRST:])
+        hum_high = held([P, BLOCKS, HALF], F32, "hum_high", tag="table2")
+        nc.sync.dma_start(hum_high[:], hum_rows[:, :, HALF:])
 
         def first_product(b, j0):
             codes, scales = w1q[b]
@@ -224,21 +224,33 @@ def tile_list_membrane_drying_page_kernel(
                 nc.scalar.copy(grouped_words[:, n0 : n0 + 2, :, :], bank[:].rearrange("p n u j -> p n j u"))
             return grouped
 
-        got_first = held([P, BLOCKS, FIRST], F32, "got_first", tag="h2")
-        size_first = held([P, BLOCKS, FIRST], F32, "size_first")
-        turned_first = held([P, FIRST // P, 2, P, 2], BF16, "turned_first", tag="table1")
-        for b in range(BLOCKS):
-            if b == BLOCKS - 1:
-                put(b, idx2, h_whole[b][:], wgs_sb, 0, S)
-            fetch(got_first[:, b, :], b, 0, FIRST)
-            nc.scalar.activation(size_first[:, b, :], got_first[:, b, :], ACT.Abs)
-            join(size_first[:, b, :], hum_first[:, b, :], turned_first, b)
-        got_low = held([P, BLOCKS - 1, REST], F32, "got_low", tag="h3")
-        for b in range(BLOCKS - 1):
-            fetch(got_low[:, b, :], b, FIRST, J)
-        x_first = quantize(turn_back(turned_first, "grouped_first")[:], "x_first")
-        got_high = held([P, REST], F32, "got_high", tag="grouped_first")
-        fetch(got_high[:], BLOCKS - 1, FIRST, J)
+        last = BLOCKS - 1
+        got_low = held([P, last, HALF], F32, "got_low", tag="h2")
+        size_low = held([P, BLOCKS, HALF], F32, "size_low", tag="table1")
+        turned_first = held([P, RUN // P, 2, P, 2], BF16, "turned_first")
+        turned_mid = held([P, RUN // P, 2, P, 2], BF16, "turned_mid")
+        for b in range(last):
+            fetch(got_low[:, b, :], b, 0, HALF)
+            nc.scalar.activation(size_low[:, b, :], got_low[:, b, :], ACT.Abs)
+            join(size_low[:, b, :RUN], hum_low[:, b, :RUN], turned_first, b)
+            join(size_low[:, b, RUN:], hum_low[:, b, RUN:], turned_mid, b)
+        put(last, idx2, h_whole[last][:], wgs_sb, 0, S)
+        got_low_last = held([P, HALF], F32, "got_low_last", tag="h_low0")
+        for j0 in (0, RUN):
+            fetch(got_low_last[:, j0 : j0 + RUN], last, j0, j0 + RUN)
+        got_high = held([P, last, HALF], F32, "got_high", tag="h3")
+        for b in range(last):
+            fetch(got_high[:, b, :], b, HALF, J)
+
+        def finish_x(j0, turned, name):
+            cols = slice(j0, j0 + RUN)
+            nc.scalar.activation(size_low[:, last, cols], got_low_last[:, cols], ACT.Abs)
+            join(size_low[:, last, cols], hum_low[:, last, cols], turned, last)
+            return quantize(turn_back(turned, "grouped_" + name)[:], "x_" + name)
+
+        x_first = finish_x(0, turned_first, "first")
+        got_high_last = held([P, HALF], F32, "got_high_last", tag="grouped_first")
+        fetch(got_high_last[:], last, HALF, J)
 
         def product_a(dest, x, b):
             nc.tensor.matmul_mx(
@@ -281,31 +293,40 @@ def tile_list_membrane_drying_page_kernel(
             ya_sb, yb = pair
             nc.vector.scalar_tensor_tensor(y, yb, bias[:, BLOCKS + b : BLOCKS + b + 1], ya_sb[:], ALU.add, ALU.max)
 
-        size_rest = held([P, BLOCKS, REST], F32, "size_rest", tag="table1")
+        def rewrite_pair(blocks, pairs, y, j0, j1):
+            for i, b in enumerate(blocks):
+                larger(y[:, i, :], pairs[b], b)
+            for i, b in enumerate(blocks):
+                put(b, idx4, y[:, i, :], wgo_sb, j0, j1)
 
-        def make_x(j0, j1, name):
-            cols = slice(j0 - FIRST, j1 - FIRST)
-            turned = held([P, (j1 - j0) // P, 2, P, 2], BF16, "turned_" + name)
+        def make_x_end():
+            size_high = held([P, BLOCKS, HALF], F32, "size_high", tag="turned_mid")
+            turned_end = held([P, HALF // P, 2, P, 2], BF16, "turned_end")
             for b in range(BLOCKS):
-                got = got_low[:, b, cols] if b < BLOCKS - 1 else got_high[:, cols]
-                nc.scalar.activation(size_rest[:, b, cols], got, ACT.Abs)
-                join(size_rest[:, b, cols], hum_rest[:, b, cols], turned, b)
-            return quantize(turn_back(turned, "grouped_" + name)[:], "x_" + name)
+                got = got_high[:, b, :] if b < last else got_high_last[:]
+                nc.scalar.activation(size_high[:, b, :], got, ACT.Abs)
+                join(size_high[:, b, :], hum_high[:, b, :], turned_end, b)
+            return quantize(turn_back(turned_end, "grouped_end")[:], "x_end")
 
-        x = x_first
-        for j0, j1, j2, name in ((0, FIRST, 2 * FIRST, "mid"), (FIRST, 2 * FIRST, J, "end")):
-            for b in range(BLOCKS - 1):
-                y = ring.tile([P, j1 - j0], F32, name="y_early")
-                larger(y[:], scores(x, b), b)
-                put(b, idx4, y[:], wgo_sb, j0, j1)
-            last = scores(x, BLOCKS - 1)
-            x = make_x(j1, j2, name)
-            y = held([P, j1 - j0], F32, "y_before_" + name, tag="grouped_" + name)
-            larger(y[:], last, BLOCKS - 1)
-            put(BLOCKS - 1, idx4, y[:], wgo_sb, j0, j1)
+        pairs = [scores(x_first, b) for b in range(BLOCKS)]
+        y = held([P, 2, RUN], F32, "y_first")
+        rewrite_pair((0, 1), pairs, y, 0, RUN)
+        x_mid = finish_x(RUN, turned_mid, "mid")
+        y = held([P, 2, RUN], F32, "y_first_late", tag="grouped_mid")
+        rewrite_pair((2, 3), pairs, y, 0, RUN)
 
+        pairs = [scores(x_mid, b) for b in range(BLOCKS)]
+        y = held([P, 2, RUN], F32, "y_mid", tag="y_first")
+        rewrite_pair((0, 1), pairs, y, RUN, HALF)
+        x_end = make_x_end()
+        y = held([P, 2, RUN], F32, "y_mid_late", tag="grouped_end")
+        rewrite_pair((2, 3), pairs, y, RUN, HALF)
+
+        pairs = [scores(x_end, b) for b in range(BLOCKS)]
+        y = held([P, BLOCKS, HALF], F32, "y_end", tag="table1")
+        larger(y[:, 0, :], pairs[0], 0)
         for b in range(BLOCKS):
-            y = ring.tile([P, J - 2 * FIRST], F32, name="y_late")
-            larger(y[:], scores(x, b), b)
-            put(b, idx4, y[:], wgo_sb, 2 * FIRST, J)
+            if b < last:
+                larger(y[:, b + 1, :], pairs[b + 1], b + 1)
+            put(b, idx4, y[:, b, :], wgo_sb, HALF, J)
             nc.sync.dma_start(out[P * b : P * (b + 1), :], page[b][:])

from contextlib import ExitStack

import concourse.mybir as mybir
from concourse.masks import make_identity

K, H, T, S, T2, J = 1536, 512, 4096, 1024, 2048, 1024
FLOPS = 2 * K * H * S + 2 * 2 * H * H * J

F32 = mybir.dt.float32
BF16 = mybir.dt.bfloat16
I32 = mybir.dt.int32
U32 = mybir.dt.uint32
U16 = mybir.dt.uint16
U8 = mybir.dt.uint8
FP8X4 = mybir.dt.float8_e4m3fn_x4
FP4X4 = mybir.dt.float4_e2m1fn_x4
ALU = mybir.AluOpType
ACT = mybir.ActivationFunctionType

P = 128
PASSES = K // 512
BLOCKS = H // P
HALF = S // 2
RUN = 256


def tile_list_membrane_drying_page_kernel(
    tc, tab_words, tab_scales, offs, offs2, offs3, offs4, w1, b1, page0, wgs, hum, wa_words, wa_scales, wb, b2, wgo, out
):
    nc = tc.nc
    with ExitStack() as ctx:
        lists = ctx.enter_context(tc.tile_pool(name="lists", bufs=1))
        keep = ctx.enter_context(tc.tile_pool(name="keep", bufs=1))
        ring = ctx.enter_context(tc.tile_pool(name="ring", bufs=4))
        acc_pool = ctx.enter_context(tc.psum_pool(name="acc", bufs=4))
        turn_pool = ctx.enter_context(tc.psum_pool(name="turn", bufs=2))

        def held(shape, dtype, name, tag=None):
            return keep.tile(shape, dtype, name=name, tag=tag or name, align_bytes=64)

        def load_list(source, name):
            tile = lists.tile([P, S // 16], U16, name=name)
            nc.sync.dma_start(tile[:], source)
            return tile

        def entries(list_tile, start, stop):
            return list_tile[:, start // 16 : stop // 16]

        def load_table(a):
            tile = held([P, T], U32, f"table{a}")
            nc.sync.dma_start(tile[:].bitcast(I32), tab_words[a].rearrange("p n t -> p (n t)").bitcast(I32))
            return tile

        def load_w1(c0, c1):
            tiles = []
            for a in range(PASSES):
                tile = held([P, 4, c1 - c0], F32, f"w1raw{c0}_{a}")
                nc.sync.dma_start(tile[:], w1[512 * a : 512 * (a + 1), c0:c1].rearrange("(p j) c -> p j c", j=4))
                tiles.append(tile)
            return tiles

        def load_page(b):
            tile = held([P, T2], F32, f"page{b}")
            nc.sync.dma_start(tile[:], page0[P * b : P * (b + 1), :])
            return tile

        identity = held([P, P], F32, "identity")
        make_identity(nc, identity[:])
        table_scales = held([P, T], U8, "table_scales")
        nc.vector.memset(table_scales[:].bitcast(I32), 0)
        for q in range(4):
            nc.gpsimd.dma_start(
                table_scales[32 * q : 32 * q + 4 * PASSES, :].bitcast(I32), tab_scales[:, 4 * q : 4 * q + 4, :].bitcast(I32)
            )
        bias_rows = held([P, P], F32, "bias_rows")
        nc.vector.memset(bias_rows[:], 0.0)
        wa_scale = held([P, H], U8, "wa_scale")
        nc.vector.memset(wa_scale[:].bitcast(I32), 0)

        idx = load_list(offs, "idx")
        table = [load_table(0)]
        w1_raw0 = load_w1(0, P)
        table.append(load_table(1))
        table.append(load_table(2))
        wgs_sb = held([P, S], F32, "wgs_sb")
        nc.sync.dma_start(wgs_sb[:, :HALF], wgs[:, :HALF])
        page = [load_page(0)]
        nc.scalar.dma_start(bias_rows[0:BLOCKS, :], b1.rearrange("(b p) -> b p", p=P))
        nc.scalar.dma_start(bias_rows[BLOCKS : 2 * BLOCKS, :], b2.rearrange("(b p) -> b p", p=P))
        idx2 = load_list(offs2, "idx2")
        w1_raw1 = load_w1(P, 2 * P)
        nc.sync.dma_start(wgs_sb[:, HALF:], wgs[:, HALF:])
        page.append(load_page(1))
        w1_raw23 = load_w1(2 * P, 4 * P)

        bias_bank = turn_pool.tile([P, P], F32, name="bias_bank", tag="back")
        nc.tensor.transpose(bias_bank[:], bias_rows[:], identity[:])
        bias = held([P, 2 * BLOCKS], F32, "bias")
        nc.scalar.copy(bias[:], bias_bank[:, : 2 * BLOCKS])

        def round_w1(raw, name):
            n = raw[0].shape[2] // P
            grouped = held([P, n, PASSES, 4 * P], BF16, name)
            for a in range(PASSES):
                nc.scalar.copy(
                    grouped[:, :, a, :].rearrange("p n (c i j) -> p n c j i", i=4, j=4),
                    raw[a][:].rearrange("p j (n c i) -> p n c j i", n=n, i=4),
                )
            return grouped

        def quantize(source, name):
            width = source.shape[1] // 4
            codes = held([P, width], U32, name + "_codes")
            scales = held([P, width], U8, name + "_scales")
            nc.vector.quantize_mx(out=codes[:].bitcast(FP8X4), scales=scales[:], in_=source)
            return codes, scales

        def quantize_w1(grouped, n, name):
            return quantize(grouped[:, n, :, :].rearrange("p a w -> p (a w)"), name)

        picked = [held([P, S], U32, f"picked{a}") for a in range(PASSES - 1)]
        picked_scales = held([P, S], U8, "picked_scales")
        w1q = [quantize_w1(round_w1(w1_raw0, "w1grp0"), 0, "w1q0")]
        nc.vector.tensor_copy(picked[0][:], table[0][:].indirect(idx[:]))
        nc.vector.tensor_copy(picked[1][:], table[1][:].indirect(idx[:]))
        nc.vector.tensor_copy(picked_scales[:], table_scales[:].indirect(idx[:]))
        picked.append(held([P, S], U32, "picked2", tag="table_scales"))
        for j0 in (0, HALF):
            nc.vector.tensor_copy(picked[2][:, j0 : j0 + HALF], table[2][:].indirect(entries(idx, j0, j0 + HALF)))

        wb_raw = held([P, 4, H], F32, "wb_raw", tag="table0")
        nc.sync.dma_start(wb_raw[:], wb.rearrange("(p j) c -> p j c", j=4))
        idx3 = load_list(offs3, "idx3")
        page.append(load_page(2))
        hum_rows = hum.rearrange("(b p) j -> p b j", p=P)
        hum_low = held([P, BLOCKS, HALF], F32, "hum_low")
        nc.sync.dma_start(hum_low[:], hum_rows[:, :, :HALF])
        page.append(load_page(3))
        idx4 = load_list(offs4, "idx4")
        wa_codes = held([P, 2 * H], U8, "wa_codes")
        nc.sync.dma_start(wa_codes[:].bitcast(I32), wa_words[0].bitcast(I32))
        for q in range(4):
            nc.sync.dma_start(wa_scale[32 * q : 32 * q + 4, :].bitcast(I32), wa_scales[0, 4 * q : 4 * q + 4, :].bitcast(I32))
        wgo_sb = held([P, J], F32, "wgo_sb")
        nc.sync.dma_start(wgo_sb[:], wgo)
        hum_high = held([P, BLOCKS, HALF], F32, "hum_high", tag="table2")
        nc.sync.dma_start(hum_high[:], hum_rows[:, :, HALF:])

        def first_product(b, j0):
            codes, scales = w1q[b]
            acc = acc_pool.tile([P, HALF], F32, name="acc")
            for a in range(PASSES):
                nc.tensor.matmul_mx(
                    out=acc[:],
                    lhsT=codes[:, P * a : P * (a + 1)].bitcast(FP8X4),
                    lhsT_scale=scales[:, P * a : P * (a + 1)],
                    rhs=picked[a][:, j0 : j0 + HALF].bitcast(FP8X4),
                    rhs_scale=picked_scales[4 * a :, j0 : j0 + HALF],
                    start=(a == 0),
                    stop=(a == PASSES - 1),
                )
            return acc

        def add_b1(h, acc, b):
            nc.scalar.activation(h, acc[:], ACT.Identity, bias=bias[:, b : b + 1])

        def put(b, list_tile, values, weights, j0, j1):
            nc.vector.tensor_tensor(page[b][:].indirect(entries(list_tile, j0, j1)), values, weights[:, j0:j1], ALU.mult)

        for b, raw, c0 in ((0, w1_raw1, P), (1, w1_raw23, 2 * P)):
            low, high = first_product(b, 0), first_product(b, HALF)
            h_low = held([P, HALF], F32, f"h_low{b}")
            add_b1(h_low[:], low, b)
            put(b, idx2, h_low[:], wgs_sb, 0, HALF)
            grouped = round_w1(raw, f"w1grp{c0}")
            for n in range(grouped.shape[1]):
                w1q.append(quantize_w1(grouped, n, f"w1q{len(w1q)}"))
            h_high = held([P, HALF], F32, f"h_high{b}", tag=f"w1raw{c0}_{PASSES - 1}")
            add_b1(h_high[:], high, b)
            put(b, idx2, h_high[:], wgs_sb, HALF, S)

        h_whole = {}
        for b in (2, 3):
            h_whole[b] = held([P, S], F32, f"h{b}")
            for j0 in (0, HALF):
                add_b1(h_whole[b][:, j0 : j0 + HALF], first_product(b, j0), b)

        wb_grouped = held([P, H, 4], BF16, "wb_grouped")
        for b in range(BLOCKS):
            nc.scalar.copy(
                wb_grouped[:, P * b : P * (b + 1), :].rearrange("p (c i) j -> p c j i", i=4),
                wb_raw[:, :, P * b : P * (b + 1)].rearrange("p j (c i) -> p c j i", i=4),
            )
        wb_codes, wb_scales = quantize(wb_grouped[:].rearrange("p c j -> p (c j)"), "wbq")

        put(2, idx2, h_whole[2][:], wgs_sb, 0, S)

        def fetch(dest, b, j0, j1):
            nc.vector.tensor_copy(dest, page[b][:].indirect(entries(idx3, j0, j1)))

        def join(size, humidity, turned, b):
            n = size.shape[1] // P
            bank = turn_pool.tile([P, n, P], F32, name="sum_bank", tag="sum")
            for jb in range(n):
                cols = slice(P * jb, P * (jb + 1))
                nc.tensor.matmul(bank[:, jb, :], humidity[:, cols], identity[:], start=True, stop=False, is_transpose=True)
                nc.tensor.matmul(bank[:, jb, :], size[:, cols], identity[:], start=False, stop=True, is_transpose=True)
            nc.scalar.copy(
                turned[:, :, :, 32 * b : 32 * (b + 1), :],
                bank[:].rearrange("j n (q u e) -> j n u q e", u=2, e=2),
            )

        def turn_back(turned, name):
            n = turned.shape[1]
            words = turned[:].rearrange("j n u q e -> j (n u q e)").bitcast(F32)
            grouped = held([P, n * P * 4], BF16, name)
            grouped_words = grouped[:].bitcast(F32).rearrange("p (n j u) -> p n j u", j=P, u=2)
            for n0 in range(0, n, 2):
                bank = turn_pool.tile([P, 2, 2, P], F32, name="back_bank", tag="back")
                for jb in range(2):
                    for u in range(2):
                        w0 = ((n0 + jb) * 2 + u) * P
                        nc.tensor.transpose(bank[:, jb, u, :], words[:, w0 : w0 + P], identity[:])
                nc.scalar.copy(grouped_words[:, n0 : n0 + 2, :, :], bank[:].rearrange("p n u j -> p n j u"))
            return grouped

        last = BLOCKS - 1
        got_low = held([P, last, HALF], F32, "got_low", tag="h2")
        size_low = held([P, BLOCKS, HALF], F32, "size_low", tag="table1")
        turned_first = held([P, RUN // P, 2, P, 2], BF16, "turned_first")
        turned_mid = held([P, RUN // P, 2, P, 2], BF16, "turned_mid")
        for b in range(last):
            fetch(got_low[:, b, :], b, 0, HALF)
            nc.scalar.activation(size_low[:, b, :], got_low[:, b, :], ACT.Abs)
            join(size_low[:, b, :RUN], hum_low[:, b, :RUN], turned_first, b)
            join(size_low[:, b, RUN:], hum_low[:, b, RUN:], turned_mid, b)
        put(last, idx2, h_whole[last][:], wgs_sb, 0, S)
        got_low_last = held([P, HALF], F32, "got_low_last", tag="h_low0")
        for j0 in (0, RUN):
            fetch(got_low_last[:, j0 : j0 + RUN], last, j0, j0 + RUN)
        got_high = held([P, last, HALF], F32, "got_high", tag="h3")
        for b in range(last):
            fetch(got_high[:, b, :], b, HALF, J)

        def finish_x(j0, turned, name):
            cols = slice(j0, j0 + RUN)
            nc.scalar.activation(size_low[:, last, cols], got_low_last[:, cols], ACT.Abs)
            join(size_low[:, last, cols], hum_low[:, last, cols], turned, last)
            return quantize(turn_back(turned, "grouped_" + name)[:], "x_" + name)

        x_first = finish_x(0, turned_first, "first")
        got_high_last = held([P, HALF], F32, "got_high_last", tag="grouped_first")
        fetch(got_high_last[:], last, HALF, J)

        def product_a(dest, x, b):
            nc.tensor.matmul_mx(
                out=dest,
                lhsT=wa_codes[:, 2 * P * b : 2 * P * (b + 1)].bitcast(FP4X4),
                lhsT_scale=wa_scale[:, P * b : P * (b + 1)],
                rhs=x[0][:].bitcast(FP8X4),
                rhs_scale=x[1][:],
                start=True,
                stop=True,
            )

        def product_b(dest, x, b):
            nc.tensor.matmul_mx(
                out=dest,
                lhsT=wb_codes[:, P * b : P * (b + 1)].bitcast(FP8X4),
                lhsT_scale=wb_scales[:, P * b : P * (b + 1)],
                rhs=x[0][:].bitcast(FP8X4),
                rhs_scale=x[1][:],
                start=True,
                stop=True,
            )

        def scores(x, b):
            width = x[0].shape[1]
            if 2 * width <= 512:
                bank = acc_pool.tile([P, 2, width], F32, name="acc")
                ya, yb = bank[:, 0, :], bank[:, 1, :]
            else:
                bank_a = acc_pool.tile([P, width], F32, name="acc")
                bank_b = acc_pool.tile([P, width], F32, name="acc")
                ya, yb = bank_a[:], bank_b[:]
            product_a(ya, x, b)
            product_b(yb, x, b)
            ya_sb = ring.tile([P, width], F32, name=f"ya_sb{width}")
            nc.scalar.activation(ya_sb[:], ya, ACT.Identity, bias=bias[:, BLOCKS + b : BLOCKS + b + 1])
            return ya_sb, yb

        def larger(y, pair, b):
            ya_sb, yb = pair
            nc.vector.scalar_tensor_tensor(y, yb, bias[:, BLOCKS + b : BLOCKS + b + 1], ya_sb[:], ALU.add, ALU.max)

        def rewrite_pair(blocks, pairs, y, j0, j1):
            for i, b in enumerate(blocks):
                larger(y[:, i, :], pairs[b], b)
            for i, b in enumerate(blocks):
                put(b, idx4, y[:, i, :], wgo_sb, j0, j1)

        def make_x_end():
            size_high = held([P, BLOCKS, HALF], F32, "size_high", tag="turned_mid")
            turned_end = held([P, HALF // P, 2, P, 2], BF16, "turned_end")
            for b in range(BLOCKS):
                got = got_high[:, b, :] if b < last else got_high_last[:]
                nc.scalar.activation(size_high[:, b, :], got, ACT.Abs)
                join(size_high[:, b, :], hum_high[:, b, :], turned_end, b)
            return quantize(turn_back(turned_end, "grouped_end")[:], "x_end")

        pairs = [scores(x_first, b) for b in range(BLOCKS)]
        y = held([P, 2, RUN], F32, "y_first")
        rewrite_pair((0, 1), pairs, y, 0, RUN)
        x_mid = finish_x(RUN, turned_mid, "mid")
        y = held([P, 2, RUN], F32, "y_first_late", tag="grouped_mid")
        rewrite_pair((2, 3), pairs, y, 0, RUN)

        pairs = [scores(x_mid, b) for b in range(BLOCKS)]
        y = held([P, 2, RUN], F32, "y_mid", tag="y_first")
        rewrite_pair((0, 1), pairs, y, RUN, HALF)
        x_end = make_x_end()
        y = held([P, 2, RUN], F32, "y_mid_late", tag="grouped_end")
        rewrite_pair((2, 3), pairs, y, RUN, HALF)

        pairs = [scores(x_end, b) for b in range(BLOCKS)]
        y = held([P, BLOCKS, HALF], F32, "y_end", tag="table1")
        larger(y[:, 0, :], pairs[0], 0)
        for b in range(BLOCKS):
            if b < last:
                larger(y[:, b + 1, :], pairs[b + 1], b + 1)
            put(b, idx4, y[:, b, :], wgo_sb, HALF, J)
            nc.sync.dma_start(out[P * b : P * (b + 1), :], page[b][:])
